import numpy as np
import ml_dtypes


def mxq(x, axis, fmt="e4m3"):
    dtype, down = {"e4m3": (ml_dtypes.float8_e4m3fn, 7), "e5m2": (ml_dtypes.float8_e5m2, 14)}[fmt]
    v = np.moveaxis(np.asarray(x, np.float32).astype(ml_dtypes.bfloat16).astype(np.float64), axis, -1)
    blocks = v.reshape(v.shape[:-1] + (-1, 32))
    amax = np.abs(blocks).max(-1, keepdims=True)
    byte = np.maximum(np.where(amax > 0, np.frexp(amax)[1] - 1 + 127, 0) - down, 1)
    scale = np.exp2(byte - 127.0)
    codes = (blocks / scale).astype(np.float32).astype(dtype).astype(np.float64)
    return np.moveaxis((codes * scale).reshape(v.shape), -1, axis)


WIDE = False


def mx_kscale(k):
    if not WIDE:
        return np.ones(k)
    levels = np.array([24, -24, 12, -12, 0])
    if k % 512:
        return np.exp2(np.random.permutation(np.resize(levels, k // 32))).repeat(32)
    a = np.empty((k // 512, 16))
    for p in range(k // 512):
        a[p, :8] = np.random.permutation(np.resize(levels, 8))
        for g in range(8):
            far = levels[np.abs(levels - a[p, g]) >= 10]
            a[p, g + 8] = far[np.random.randint(len(far))]
    return np.exp2(a.ravel()).repeat(32)


def f64(x):
    return np.asarray(x).astype(np.float64)


def striped(idx):
    return np.tile(idx.reshape(-1, 16).T, (8, 1)).astype(np.uint16)


def unstriped(offs):
    return offs[:16].T.reshape(-1).astype(np.int64)


E2M1 = np.array([0.0, 0.5, 1.0, 1.5, 2.0, 3.0, 4.0, 6.0, -0.0, -0.5, -1.0, -1.5, -2.0, -3.0, -4.0, -6.0])


def pack_weight(w, fmt):
    k, n = w.shape
    w = f64(np.asarray(w, np.float32).astype(ml_dtypes.bfloat16)).reshape(k // 32, 32, n)
    amax = np.abs(w).max(1)
    if fmt == "e4m3":
        byte = np.frexp(amax)[1] - 1 + 127 - 7
    else:
        mant, ex = np.frexp(amax / 6.0)
        byte = np.where(mant > 0.5, ex, ex - 1) + 127
    byte = np.clip(np.where(amax > 0, byte, 1), 1, 254)
    scaled = (w * np.exp2(127.0 - byte)[:, None, :]).reshape(k, n).astype(np.float32)
    by_word = np.ascontiguousarray(scaled.reshape(k // 512, 128, 4, n).transpose(0, 1, 3, 2))
    if fmt == "e4m3":
        words = by_word.astype(ml_dtypes.float8_e4m3fn).view(np.uint8)
    else:
        c = by_word.astype(ml_dtypes.float4_e2m1fn).view(np.uint8) & 0xF
        words = (c[..., 0::2] | (c[..., 1::2] << 4)).reshape(k // 512, 128, 2 * n)
    return np.ascontiguousarray(words), np.ascontiguousarray(byte.astype(np.uint8).reshape(k // 512, 16, n))


def unpack_weight(words, scales, fmt):
    g, _, n = scales.shape
    words = np.ascontiguousarray(words).reshape(g, 128, n, -1)
    if fmt == "e4m3":
        vals = words.view(ml_dtypes.float8_e4m3fn).astype(np.float64)
    else:
        nib = np.empty((g, 128, n, 4), np.uint8)
        nib[..., 0::2] = words & 0xF
        nib[..., 1::2] = words >> 4
        vals = E2M1[nib]
    vals = vals * np.repeat(np.exp2(scales.astype(np.float64) - 127.0), 8, axis=1)[..., None]
    return vals.transpose(0, 1, 3, 2).reshape(g * 512, n)


def split(x):
    m, e = np.frexp(f64(x))
    hi = np.ldexp(np.trunc(16.0 * m) / 16.0, e)
    return hi, f64(x) - hi


def sigm(f):
    return 1.0 / (1.0 + np.exp(-np.maximum(f, -700.0)))


K, N, T, J = 512, 1024, 2048, 1024


def setup_inputs():
    n = np.random.standard_normal
    s = mx_kscale(K)[:, None]
    p_tab = pack_weight(n((K, T)) * s, "e4m3")
    p_wk = pack_weight(n((K, N)) / np.sqrt(K) / s, "e2m1")
    return {
        "tab_words": p_tab[0],
        "tab_scales": p_tab[1],
        "wk_words": p_wk[0],
        "wk_scales": p_wk[1],
        "wv": (n((K, N)) / np.sqrt(K) / s).astype(np.float32),
        "st": (n((N, J))).astype(np.float32),
        "res": (n((N, J))).astype(np.float32),
        "offs": striped(np.random.permutation(T)[:J]),
    }


def reference(tab_words, tab_scales, wk_words, wk_scales, wv, st, res, offs):
    idx = unstriped(offs)
    tab_ = unpack_weight(tab_words, tab_scales, "e4m3")[:, idx]
    wk_ = unpack_weight(wk_words, wk_scales, "e2m1")
    wv_hi, wv_lo = split(wv)
    wv_hi_, wv_lo_ = mxq(wv_hi, 0, "e4m3"), mxq(wv_lo, 0, "e4m3")
    ke = wk_.T @ tab_
    ve = wv_hi_.T @ tab_ + wv_lo_.T @ tab_
    gate = sigm(ke + f64(st))
    return f64(res) + gate * ve

@@ -1,0 +1,171 @@
+from contextlib import ExitStack
+
+import concourse.mybir as mybir
+
+K, N, T, J = 512, 1024, 2048, 1024
+FLOPS = 3 * 2 * K * N * J
+
+F32 = mybir.dt.float32
+BF16 = mybir.dt.bfloat16
+I32 = mybir.dt.int32
+U32 = mybir.dt.uint32
+U16 = mybir.dt.uint16
+U8 = mybir.dt.uint8
+FP8X4 = mybir.dt.float8_e4m3fn_x4
+FP4X4 = mybir.dt.float4_e2m1fn_x4
+ALU = mybir.AluOpType
+ACT = mybir.ActivationFunctionType
+
+P = 128
+PACK = 4
+BANK = 512
+N_TILES = N // P
+HALF = N // 2
+KEEP_TWO_HI = 0xFFF0FFF0 - (1 << 32)
+
+
+def load_scale_rows(nc, plane, scales):
+    rows = scales[0].bitcast(I32)
+    for q in range(4):
+        nc.sync.dma_start(out=plane[32 * q : 32 * q + 4, :], in_=rows[4 * q : 4 * q + 4, :])
+
+
+def tile_list_engram_hl_add_kernel(
+    tc, tab_words, tab_scales, wk_words, wk_scales, wv, st, res, offs, out
+):
+    nc = tc.nc
+    with ExitStack() as ctx:
+        keep = ctx.enter_context(tc.tile_pool(name="keep", bufs=1))
+        ring = ctx.enter_context(tc.tile_pool(name="ring", bufs=4))
+        psum = ctx.enter_context(tc.psum_pool(name="psum", bufs=4))
+
+        offsets = keep.tile([P, J // 16], U16, name="offsets")
+        table = keep.tile([P, T], I32, name="table", align_bytes=64)
+        table_sc = keep.tile([P, T // 4], I32, name="table_sc", align_bytes=64)
+        wk_codes = keep.tile([P, N // 2], I32, name="wk_codes", align_bytes=64)
+        wk_sc = keep.tile([P, N // 4], I32, name="wk_sc", align_bytes=64)
+        nc.vector.memset(table_sc[:], 0)
+        nc.vector.memset(wk_sc[:], 0)
+
+        nc.sync.dma_start(offsets[:], offs)
+        nc.sync.dma_start(out=table[:], in_=tab_words[0].rearrange("p t i -> p (t i)").bitcast(I32))
+        load_scale_rows(nc, table_sc, tab_scales)
+        wv_rows = wv.rearrange("(p i) n -> p i n", i=PACK)
+        wv_raw = []
+        for h in range(2):
+            raw = keep.tile([P, PACK, HALF], F32, name="wv_raw%d" % h)
+            nc.sync.dma_start(out=raw[:], in_=wv_rows[:, :, h * HALF : (h + 1) * HALF])
+            wv_raw.append(raw)
+        nc.sync.dma_start(out=wk_codes[:], in_=wk_words[0].bitcast(I32))
+        load_scale_rows(nc, wk_sc, wk_scales)
+        st_sb, res_sb = [], []
+        for pair in range(N_TILES // 2):
+            rows = slice(2 * P * pair, 2 * P * (pair + 1))
+            st_pair = keep.tile([P, 2, J], F32, name="st%d" % pair)
+            res_pair = keep.tile([P, 2, J], F32, name="res%d" % pair)
+            nc.sync.dma_start(out=st_pair[:], in_=st[rows, :].rearrange("(r p) j -> p r j", p=P))
+            nc.sync.dma_start(out=res_pair[:], in_=res[rows, :].rearrange("(r p) j -> p r j", p=P))
+            st_sb.extend([st_pair[:, 0, :], st_pair[:, 1, :]])
+            res_sb.extend([res_pair[:, 0, :], res_pair[:, 1, :]])
+
+        picked = keep.tile([P, J], U32, name="picked", align_bytes=64)
+        picked_sc = keep.tile([P, J], U8, name="picked_sc", align_bytes=64)
+        nc.vector.tensor_copy(picked[:], table[:].bitcast(U32).indirect(offsets[:]))
+        nc.vector.tensor_copy(picked_sc[:], table_sc[:].bitcast(U8).indirect(offsets[:]))
+
+        tops, his, los = [], [], []
+        for h in range(2):
+            top = keep.tile([P, HALF * PACK], BF16, name="top%d" % h, align_bytes=64)
+            upper = wv_raw[h][:].bitcast(BF16)[:, :, 1::2]
+            nc.scalar.copy(
+                out=top[:].rearrange("p (c u i) -> p c i u", u=4, i=PACK),
+                in_=upper.rearrange("p i (c u) -> p c i u", u=4),
+            )
+            tops.append(top)
+            his.append(keep.tile([P, HALF * PACK], BF16, name="hi%d" % h, align_bytes=64))
+            los.append(keep.tile([P, HALF * PACK], BF16, name="lo%d" % h, align_bytes=64))
+
+        codes, planes = {}, {}
+        for part in ("hi", "lo"):
+            for h in range(2):
+                codes[part, h] = keep.tile([P, HALF], U32, name="codes_%s%d" % (part, h), align_bytes=64)
+                planes[part, h] = keep.tile([P, HALF], U8, name="plane_%s%d" % (part, h), align_bytes=64)
+
+        def mask(h):
+            nc.vector.tensor_scalar(
+                out=his[h][:].bitcast(I32), in0=tops[h][:].bitcast(I32),
+                scalar1=KEEP_TWO_HI, scalar2=None, op0=ALU.bitwise_and,
+            )
+
+        def rest(h):
+            nc.vector.tensor_tensor(
+                out=los[h][:].rearrange("p (c u i) -> p c i u", u=4, i=PACK),
+                in0=wv_raw[h][:].rearrange("p i (c u) -> p c i u", u=4),
+                in1=his[h][:].rearrange("p (c u i) -> p c i u", u=4, i=PACK),
+                op=ALU.subtract,
+            )
+
+        def quantize(part, h):
+            source = his[h] if part == "hi" else los[h]
+            nc.vector.quantize_mx(out=codes[part, h][:].bitcast(FP8X4), scales=planes[part, h][:], in_=source[:])
+
+        mask(0)
+        rest(0)
+        quantize("hi", 0)
+        mask(1)
+        quantize("lo", 0)
+        rest(1)
+        quantize("hi", 1)
+        quantize("lo", 1)
+
+        units = [(nt, jh) for nt in range(N_TILES) for jh in range(J // BANK)]
+        gates, values, gated, results = {}, {}, {}, {}
+
+        def front(u):
+            nt, jh = units[u]
+            js = slice(jh * BANK, (jh + 1) * BANK)
+            rhs = picked[:, js].bitcast(FP8X4)
+            rhs_sc = picked_sc[:, js]
+            key = psum.tile([P, BANK], F32, name="key")
+            nc.tensor.matmul_mx(
+                out=key[:],
+                lhsT=wk_codes[:].bitcast(U8)[:, 2 * P * nt : 2 * P * (nt + 1)].bitcast(FP4X4),
+                lhsT_scale=wk_sc[:].bitcast(U8)[:, P * nt : P * (nt + 1)],
+                rhs=rhs, rhs_scale=rhs_sc, start=True, stop=True,
+            )
+            value = psum.tile([P, BANK], F32, name="value")
+            h, c0 = divmod(nt * P, HALF)
+            for part in ("hi", "lo"):
+                nc.tensor.matmul_mx(
+                    out=value[:],
+                    lhsT=codes[part, h][:, c0 : c0 + P].bitcast(FP8X4),
+                    lhsT_scale=planes[part, h][:, c0 : c0 + P],
+                    rhs=rhs, rhs_scale=rhs_sc, start=(part == "hi"), stop=(part == "lo"),
+                )
+            logit = ring.tile([P, BANK], F32, name="logit")
+            nc.vector.tensor_tensor(out=logit[:], in0=key[:], in1=st_sb[nt][:, js], op=ALU.add)
+            gate = ring.tile([P, BANK], F32, name="gate")
+            nc.scalar.activation(out=gate[:], in_=logit[:], func=ACT.Sigmoid)
+            gates[u], values[u] = gate, value
+
+        def back(u):
+            nt, jh = units[u]
+            js = slice(jh * BANK, (jh + 1) * BANK)
+            rows = slice(nt * P, (nt + 1) * P)
+            if jh == 0:
+                gated[nt] = ring.tile([P, J], F32, name="gated")
+                results[nt] = keep.tile([P, J], F32, name="result%d" % nt)
+            nc.vector.tensor_tensor(out=gated[nt][:, js], in0=values[u][:], in1=gates[u][:], op=ALU.mult)
+            if nt == N_TILES - 1:
+                nc.vector.tensor_tensor(out=results[nt][:, js], in0=gated[nt][:, js], in1=res_sb[nt][:, js], op=ALU.add)
+                nc.sync.dma_start(out=out[rows, js], in_=results[nt][:, js])
+            elif jh == 1:
+                nc.gpsimd.tensor_tensor(out=results[nt][:], in0=gated[nt][:], in1=res_sb[nt], op=ALU.add)
+                nc.sync.dma_start(out=out[rows, :], in_=results[nt][:])
+
+        lead = 2
+        for step in range(len(units) + lead):
+            if step < len(units):
+                front(step)
+            if step >= lead:
+                back(step - lead)

@@ -21,6 +21,7 @@ PACK = 4
 BANK = 512
 N_TILES = N // P
 HALF = N // 2
+CHUNKS = ((0, 256), (256, 256), (512, 256), (768, 256))
 KEEP_TWO_HI = 0xFFF0FFF0 - (1 << 32)
 
 
@@ -37,7 +38,8 @@ def tile_list_engram_hl_add_kernel(
     with ExitStack() as ctx:
         keep = ctx.enter_context(tc.tile_pool(name="keep", bufs=1))
         ring = ctx.enter_context(tc.tile_pool(name="ring", bufs=4))
-        psum = ctx.enter_context(tc.psum_pool(name="psum", bufs=4))
+        keys = ctx.enter_context(tc.psum_pool(name="keys", bufs=3))
+        vals = ctx.enter_context(tc.psum_pool(name="vals", bufs=5))
 
         offsets = keep.tile([P, J // 16], U16, name="offsets")
         table = keep.tile([P, T], I32, name="table", align_bytes=64)
@@ -47,15 +49,13 @@ def tile_list_engram_hl_add_kernel(
         nc.vector.memset(table_sc[:], 0)
         nc.vector.memset(wk_sc[:], 0)
 
+        wv_rows = wv.rearrange("(p i) n -> p i n", i=PACK)
+        wv_raw = [keep.tile([P, PACK, HALF], F32, name="wv_raw%d" % h) for h in range(2)]
         nc.sync.dma_start(offsets[:], offs)
         nc.sync.dma_start(out=table[:], in_=tab_words[0].rearrange("p t i -> p (t i)").bitcast(I32))
         load_scale_rows(nc, table_sc, tab_scales)
-        wv_rows = wv.rearrange("(p i) n -> p i n", i=PACK)
-        wv_raw = []
-        for h in range(2):
-            raw = keep.tile([P, PACK, HALF], F32, name="wv_raw%d" % h)
-            nc.sync.dma_start(out=raw[:], in_=wv_rows[:, :, h * HALF : (h + 1) * HALF])
-            wv_raw.append(raw)
+        nc.sync.dma_start(out=wv_raw[0][:], in_=wv_rows[:, :, :HALF])
+        nc.sync.dma_start(out=wv_raw[1][:], in_=wv_rows[:, :, HALF:])
         nc.sync.dma_start(out=wk_codes[:], in_=wk_words[0].bitcast(I32))
         load_scale_rows(nc, wk_sc, wk_scales)
         st_sb, res_sb = [], []
@@ -70,77 +70,67 @@ def tile_list_engram_hl_add_kernel(
 
         picked = keep.tile([P, J], U32, name="picked", align_bytes=64)
         picked_sc = keep.tile([P, J], U8, name="picked_sc", align_bytes=64)
-        nc.vector.tensor_copy(picked[:], table[:].bitcast(U32).indirect(offsets[:]))
-        nc.vector.tensor_copy(picked_sc[:], table_sc[:].bitcast(U8).indirect(offsets[:]))
 
-        tops, his, los = [], [], []
-        for h in range(2):
-            top = keep.tile([P, HALF * PACK], BF16, name="top%d" % h, align_bytes=64)
-            upper = wv_raw[h][:].bitcast(BF16)[:, :, 1::2]
+        raws, tops, parts, codes, planes = [], [], {}, [], []
+        for c, (n0, width) in enumerate(CHUNKS):
+            h, c0 = divmod(n0, HALF)
+            raws.append(wv_raw[h][:, :, c0 : c0 + width])
+            top = keep.tile([P, width * PACK], BF16, name="top%d" % c, align_bytes=64)
+            upper = wv_raw[h][:].bitcast(BF16)[:, :, 2 * c0 + 1 : 2 * (c0 + width) : 2]
             nc.scalar.copy(
                 out=top[:].rearrange("p (c u i) -> p c i u", u=4, i=PACK),
                 in_=upper.rearrange("p i (c u) -> p c i u", u=4),
             )
             tops.append(top)
-            his.append(keep.tile([P, HALF * PACK], BF16, name="hi%d" % h, align_bytes=64))
-            los.append(keep.tile([P, HALF * PACK], BF16, name="lo%d" % h, align_bytes=64))
+            codes.append(keep.tile([P, 2 * width], U32, name="codes%d" % c, align_bytes=64))
+            planes.append(keep.tile([P, 2 * width], U8, name="plane%d" % c, align_bytes=64))
 
-        codes, planes = {}, {}
-        for part in ("hi", "lo"):
-            for h in range(2):
-                codes[part, h] = keep.tile([P, HALF], U32, name="codes_%s%d" % (part, h), align_bytes=64)
-                planes[part, h] = keep.tile([P, HALF], U8, name="plane_%s%d" % (part, h), align_bytes=64)
-
-        def mask(h):
+        def mask(c):
+            width = CHUNKS[c][1]
+            parts[c] = keep.tile([P, 2, width * PACK], BF16, name="parts%d" % c, align_bytes=64)
             nc.vector.tensor_scalar(
-                out=his[h][:].bitcast(I32), in0=tops[h][:].bitcast(I32),
+                out=parts[c][:, 0, :].bitcast(I32), in0=tops[c][:].bitcast(I32),
                 scalar1=KEEP_TWO_HI, scalar2=None, op0=ALU.bitwise_and,
             )
 
-        def rest(h):
+        def rest(c):
             nc.vector.tensor_tensor(
-                out=los[h][:].rearrange("p (c u i) -> p c i u", u=4, i=PACK),
-                in0=wv_raw[h][:].rearrange("p i (c u) -> p c i u", u=4),
-                in1=his[h][:].rearrange("p (c u i) -> p c i u", u=4, i=PACK),
+                out=parts[c][:, 1, :].rearrange("p (c u i) -> p c i u", u=4, i=PACK),
+                in0=raws[c].rearrange("p i (c u) -> p c i u", u=4),
+                in1=parts[c][:, 0, :].rearrange("p (c u i) -> p c i u", u=4, i=PACK),
                 op=ALU.subtract,
             )
 
-        def quantize(part, h):
-            source = his[h] if part == "hi" else los[h]
-            nc.vector.quantize_mx(out=codes[part, h][:].bitcast(FP8X4), scales=planes[part, h][:], in_=source[:])
-
-        mask(0)
-        rest(0)
-        quantize("hi", 0)
-        mask(1)
-        quantize("lo", 0)
-        rest(1)
-        quantize("hi", 1)
-        quantize("lo", 1)
+        def quantize(c):
+            nc.vector.quantize_mx(
+                out=codes[c][:].bitcast(FP8X4), scales=planes[c][:],
+                in_=parts[c][:].rearrange("p s x -> p (s x)"),
+            )
 
         units = [(nt, jh) for nt in range(N_TILES) for jh in range(J // BANK)]
-        gates, values, gated, results = {}, {}, {}, {}
+        gates, values, gated = {}, {}, {}
 
         def front(u):
             nt, jh = units[u]
             js = slice(jh * BANK, (jh + 1) * BANK)
             rhs = picked[:, js].bitcast(FP8X4)
             rhs_sc = picked_sc[:, js]
-            key = psum.tile([P, BANK], F32, name="key")
+            key = keys.tile([P, BANK], F32, name="key")
             nc.tensor.matmul_mx(
                 out=key[:],
                 lhsT=wk_codes[:].bitcast(U8)[:, 2 * P * nt : 2 * P * (nt + 1)].bitcast(FP4X4),
                 lhsT_scale=wk_sc[:].bitcast(U8)[:, P * nt : P * (nt + 1)],
                 rhs=rhs, rhs_scale=rhs_sc, start=True, stop=True,
             )
-            value = psum.tile([P, BANK], F32, name="value")
-            h, c0 = divmod(nt * P, HALF)
-            for part in ("hi", "lo"):
+            value = vals.tile([P, BANK], F32, name="value")
+            c = max(k for k, (n0, width) in enumerate(CHUNKS) if n0 <= nt * P)
+            n0, width = CHUNKS[c]
+            for part in range(2):
+                cols = slice(part * width + nt * P - n0, part * width + nt * P - n0 + P)
                 nc.tensor.matmul_mx(
                     out=value[:],
-                    lhsT=codes[part, h][:, c0 : c0 + P].bitcast(FP8X4),
-                    lhsT_scale=planes[part, h][:, c0 : c0 + P],
-                    rhs=rhs, rhs_scale=rhs_sc, start=(part == "hi"), stop=(part == "lo"),
+                    lhsT=codes[c][:, cols].bitcast(FP8X4), lhsT_scale=planes[c][:, cols],
+                    rhs=rhs, rhs_scale=rhs_sc, start=(part == 0), stop=(part == 1),
                 )
             logit = ring.tile([P, BANK], F32, name="logit")
             nc.vector.tensor_tensor(out=logit[:], in0=key[:], in1=st_sb[nt][:, js], op=ALU.add)
@@ -150,22 +140,46 @@ def tile_list_engram_hl_add_kernel(
 
         def back(u):
             nt, jh = units[u]
-            js = slice(jh * BANK, (jh + 1) * BANK)
-            rows = slice(nt * P, (nt + 1) * P)
             if jh == 0:
                 gated[nt] = ring.tile([P, J], F32, name="gated")
-                results[nt] = keep.tile([P, J], F32, name="result%d" % nt)
+            js = slice(jh * BANK, (jh + 1) * BANK)
             nc.vector.tensor_tensor(out=gated[nt][:, js], in0=values[u][:], in1=gates[u][:], op=ALU.mult)
-            if nt == N_TILES - 1:
-                nc.vector.tensor_tensor(out=results[nt][:, js], in0=gated[nt][:, js], in1=res_sb[nt][:, js], op=ALU.add)
-                nc.sync.dma_start(out=out[rows, js], in_=results[nt][:, js])
-            elif jh == 1:
-                nc.gpsimd.tensor_tensor(out=results[nt][:], in0=gated[nt][:], in1=res_sb[nt], op=ALU.add)
-                nc.sync.dma_start(out=out[rows, :], in_=results[nt][:])
 
-        lead = 2
-        for step in range(len(units) + lead):
-            if step < len(units):
-                front(step)
-            if step >= lead:
-                back(step - lead)
+        def finish(nt, js, engine):
+            result = keep.tile([P, js.stop - js.start], F32, name="result%d_%d" % (nt, js.start))
+            engine.tensor_tensor(out=result[:], in0=gated[nt][:, js], in1=res_sb[nt][:, js], op=ALU.add)
+            nc.sync.dma_start(out=out[nt * P : (nt + 1) * P, js], in_=result[:])
+
+        nc.vector.tensor_copy(picked[:], table[:].bitcast(U32).indirect(offsets[:]))
+        nc.vector.tensor_copy(picked_sc[:], table_sc[:].bitcast(U8).indirect(offsets[:]))
+        mask(0)
+        mask(1)
+        rest(0)
+        rest(1)
+        quantize(0)
+        mask(2)
+        quantize(1)
+        mask(3)
+        rest(2)
+        rest(3)
+        front(0)
+        quantize(2)
+        quantize(3)
+
+        halves = (slice(0, BANK), slice(BANK, J))
+        last = len(units) - 1
+        back(0)
+        finish(0, halves[0], nc.gpsimd)
+        front(1)
+        front(2)
+        for u in range(1, last + 1):
+            back(u)
+            nt, jh = units[u]
+            if nt in (0, N_TILES - 2):
+                finish(nt, halves[jh], nc.gpsimd)
+            elif nt < N_TILES - 2 and jh == 1:
+                finish(nt, slice(0, J), nc.gpsimd)
+            if u + 2 <= last:
+                front(u + 2)
+        for js in halves:
+            finish(N_TILES - 1, js, nc.vector)

@@ -78,8 +78,8 @@ def tile_list_engram_hl_add_kernel(
             top = keep.tile([P, width * PACK], BF16, name="top%d" % c, align_bytes=64)
             upper = wv_raw[h][:].bitcast(BF16)[:, :, 2 * c0 + 1 : 2 * (c0 + width) : 2]
             nc.scalar.copy(
-                out=top[:].rearrange("p (c u i) -> p c i u", u=4, i=PACK),
-                in_=upper.rearrange("p i (c u) -> p c i u", u=4),
+                out=top[:].rearrange("p (c u i) -> p c i u", u=2, i=PACK),
+                in_=upper.rearrange("p i (c u) -> p c i u", u=2),
             )
             tops.append(top)
             codes.append(keep.tile([P, 2 * width], U32, name="codes%d" % c, align_bytes=64))
@@ -95,9 +95,9 @@ def tile_list_engram_hl_add_kernel(
 
         def rest(c):
             nc.vector.tensor_tensor(
-                out=parts[c][:, 1, :].rearrange("p (c u i) -> p c i u", u=4, i=PACK),
-                in0=raws[c].rearrange("p i (c u) -> p c i u", u=4),
-                in1=parts[c][:, 0, :].rearrange("p (c u i) -> p c i u", u=4, i=PACK),
+                out=parts[c][:, 1, :].rearrange("p (c u i) -> p c i u", u=2, i=PACK),
+                in0=raws[c].rearrange("p i (c u) -> p c i u", u=2),
+                in1=parts[c][:, 0, :].rearrange("p (c u i) -> p c i u", u=2, i=PACK),
                 op=ALU.subtract,
             )
 

@@ -27,8 +27,8 @@ KEEP_TWO_HI = 0xFFF0FFF0 - (1 << 32)
 
 def load_scale_rows(nc, plane, scales):
     rows = scales[0].bitcast(I32)
-    for q in range(4):
-        nc.sync.dma_start(out=plane[32 * q : 32 * q + 4, :], in_=rows[4 * q : 4 * q + 4, :])
+    for r in range(4):
+        nc.sync.dma_start(out=plane[r:P:32, :], in_=rows[r:16:4, :])
 
 
 def tile_list_engram_hl_add_kernel(
@@ -145,10 +145,13 @@ def tile_list_engram_hl_add_kernel(
             js = slice(jh * BANK, (jh + 1) * BANK)
             nc.vector.tensor_tensor(out=gated[nt][:, js], in0=values[u][:], in1=gates[u][:], op=ALU.mult)
 
-        def finish(nt, js, engine):
-            result = keep.tile([P, js.stop - js.start], F32, name="result%d_%d" % (nt, js.start))
-            engine.tensor_tensor(out=result[:], in0=gated[nt][:, js], in1=res_sb[nt][:, js], op=ALU.add)
-            nc.sync.dma_start(out=out[nt * P : (nt + 1) * P, js], in_=result[:])
+        results = [keep.tile([P, J], F32, name="result%d" % nt) for nt in range(N_TILES)]
+
+        def add_res(nt, js, engine):
+            engine.tensor_tensor(out=results[nt][:, js], in0=gated[nt][:, js], in1=res_sb[nt][:, js], op=ALU.add)
+
+        def store(nt, js):
+            nc.sync.dma_start(out=out[nt * P : (nt + 1) * P, js], in_=results[nt][:, js])
 
         nc.vector.tensor_copy(picked[:], table[:].bitcast(U32).indirect(offsets[:]))
         nc.vector.tensor_copy(picked_sc[:], table_sc[:].bitcast(U8).indirect(offsets[:]))
@@ -167,19 +170,29 @@ def tile_list_engram_hl_add_kernel(
         quantize(3)
 
         halves = (slice(0, BANK), slice(BANK, J))
+        whole = slice(0, J)
         last = len(units) - 1
         back(0)
-        finish(0, halves[0], nc.gpsimd)
+        add_res(0, halves[0], nc.gpsimd)
         front(1)
         front(2)
-        for u in range(1, last + 1):
+        for u in range(1, last):
             back(u)
             nt, jh = units[u]
-            if nt in (0, N_TILES - 2):
-                finish(nt, halves[jh], nc.gpsimd)
-            elif nt < N_TILES - 2 and jh == 1:
-                finish(nt, slice(0, J), nc.gpsimd)
+            if u == 1:
+                add_res(0, halves[1], nc.gpsimd)
+                store(0, whole)
+            elif u == last - 3:
+                add_res(nt, halves[0], nc.gpsimd)
+                store(nt, halves[0])
+            elif u < last - 3 and jh == 1:
+                add_res(nt, whole, nc.gpsimd)
+                store(nt, whole)
             if u + 2 <= last:
                 front(u + 2)
+        add_res(N_TILES - 2, halves[1], nc.vector)
+        store(N_TILES - 2, halves[1])
+        back(last)
         for js in halves:
-            finish(N_TILES - 1, js, nc.vector)
+            add_res(N_TILES - 1, js, nc.vector)
+            store(N_TILES - 1, js)

@@ -176,7 +176,8 @@ def tile_list_engram_hl_add_kernel(
         add_res(0, halves[0], nc.gpsimd)
         front(1)
         front(2)
-        for u in range(1, last):
+        ahead = 3
+        for u in range(1, last + 1):
             back(u)
             nt, jh = units[u]
             if u == 1:
@@ -188,11 +189,10 @@ def tile_list_engram_hl_add_kernel(
             elif u < last - 3 and jh == 1:
                 add_res(nt, whole, nc.gpsimd)
                 store(nt, whole)
-            if u + 2 <= last:
-                front(u + 2)
-        add_res(N_TILES - 2, halves[1], nc.vector)
-        store(N_TILES - 2, halves[1])
-        back(last)
-        for js in halves:
-            add_res(N_TILES - 1, js, nc.vector)
-            store(N_TILES - 1, js)
+            lead = 2 if u < last - 4 else 3
+            while ahead <= min(u + lead, last):
+                front(ahead)
+                ahead += 1
+        for nt, jh in units[last - 2 :]:
+            add_res(nt, halves[jh], nc.vector)
+            store(nt, halves[jh])

@@ -22,6 +22,7 @@ BANK = 512
 N_TILES = N // P
 HALF = N // 2
 CHUNKS = ((0, 256), (256, 256), (512, 256), (768, 256))
+LOADS = ((0, 256), (256, 256), (512, 512))
 KEEP_TWO_HI = 0xFFF0FFF0 - (1 << 32)
 
 
@@ -47,16 +48,17 @@ def tile_list_engram_hl_add_kernel(
         wk_codes = keep.tile([P, N // 2], I32, name="wk_codes", align_bytes=64)
         wk_sc = keep.tile([P, N // 4], I32, name="wk_sc", align_bytes=64)
         nc.vector.memset(table_sc[:], 0)
-        nc.vector.memset(wk_sc[:], 0)
+        nc.gpsimd.memset(wk_sc[:], 0)
 
         wv_rows = wv.rearrange("(p i) n -> p i n", i=PACK)
-        wv_raw = [keep.tile([P, PACK, HALF], F32, name="wv_raw%d" % h) for h in range(2)]
+        wv_raw = [keep.tile([P, PACK, w], F32, name="wv_raw%d" % h) for h, (n0, w) in enumerate(LOADS)]
         nc.sync.dma_start(offsets[:], offs)
-        nc.sync.dma_start(out=table[:], in_=tab_words[0].rearrange("p t i -> p (t i)").bitcast(I32))
-        load_scale_rows(nc, table_sc, tab_scales)
-        nc.sync.dma_start(out=wv_raw[0][:], in_=wv_rows[:, :, :HALF])
-        nc.sync.dma_start(out=wv_raw[1][:], in_=wv_rows[:, :, HALF:])
         nc.sync.dma_start(out=wk_codes[:], in_=wk_words[0].bitcast(I32))
+        load_scale_rows(nc, table_sc, tab_scales)
+        nc.sync.dma_start(out=table[:], in_=tab_words[0].rearrange("p t i -> p (t i)").bitcast(I32))
+        nc.sync.dma_start(out=wv_raw[0][:], in_=wv_rows[:, :, 0:256])
+        nc.sync.dma_start(out=wv_raw[1][:], in_=wv_rows[:, :, 256:512])
+        nc.sync.dma_start(out=wv_raw[2][:], in_=wv_rows[:, :, 512:])
         load_scale_rows(nc, wk_sc, wk_scales)
         st_sb, res_sb = [], []
         for pair in range(N_TILES // 2):
@@ -64,16 +66,20 @@ def tile_list_engram_hl_add_kernel(
             st_pair = keep.tile([P, 2, J], F32, name="st%d" % pair)
             res_pair = keep.tile([P, 2, J], F32, name="res%d" % pair)
             nc.sync.dma_start(out=st_pair[:], in_=st[rows, :].rearrange("(r p) j -> p r j", p=P))
-            nc.sync.dma_start(out=res_pair[:], in_=res[rows, :].rearrange("(r p) j -> p r j", p=P))
+            if pair > 0:
+                nc.sync.dma_start(out=behind[0][:], in_=behind[1])
+            behind = (res_pair, res[rows, :].rearrange("(r p) j -> p r j", p=P))
             st_sb.extend([st_pair[:, 0, :], st_pair[:, 1, :]])
             res_sb.extend([res_pair[:, 0, :], res_pair[:, 1, :]])
+        nc.sync.dma_start(out=behind[0][:], in_=behind[1])
 
         picked = keep.tile([P, J], U32, name="picked", align_bytes=64)
         picked_sc = keep.tile([P, J], U8, name="picked_sc", align_bytes=64)
 
         raws, tops, parts, codes, planes = [], [], {}, [], []
         for c, (n0, width) in enumerate(CHUNKS):
-            h, c0 = divmod(n0, HALF)
+            h = min(c, 2)
+            c0 = n0 - LOADS[h][0]
             raws.append(wv_raw[h][:, :, c0 : c0 + width])
             top = keep.tile([P, width * PACK], BF16, name="top%d" % c, align_bytes=64)
             upper = wv_raw[h][:].bitcast(BF16)[:, :, 2 * c0 + 1 : 2 * (c0 + width) : 2]
@@ -153,20 +159,20 @@ def tile_list_engram_hl_add_kernel(
         def store(nt, js):
             nc.sync.dma_start(out=out[nt * P : (nt + 1) * P, js], in_=results[nt][:, js])
 
-        nc.vector.tensor_copy(picked[:], table[:].bitcast(U32).indirect(offsets[:]))
         nc.vector.tensor_copy(picked_sc[:], table_sc[:].bitcast(U8).indirect(offsets[:]))
+        nc.vector.tensor_copy(picked[:], table[:].bitcast(U32).indirect(offsets[:]))
         mask(0)
-        mask(1)
         rest(0)
-        rest(1)
+        mask(1)
         quantize(0)
+        rest(1)
         mask(2)
         quantize(1)
-        mask(3)
         rest(2)
+        mask(3)
+        quantize(2)
         rest(3)
         front(0)
-        quantize(2)
         quantize(3)
 
         halves = (slice(0, BANK), slice(BANK, J))

@@ -21,15 +21,16 @@ PACK = 4
 BANK = 512
 N_TILES = N // P
 HALF = N // 2
-CHUNKS = ((0, 256), (256, 256), (512, 256), (768, 256))
-LOADS = ((0, 256), (256, 256), (512, 512))
+CHUNKS = ((0, 256), (256, 256), (512, 256), (768, 128), (896, 128))
+LOADS = ((0, 256), (256, 256), (512, 384), (896, 128))
+LAST_PIECE = 128
 KEEP_TWO_HI = 0xFFF0FFF0 - (1 << 32)
 
 
-def load_scale_rows(nc, plane, scales):
+def load_scale_rows(queues, plane, scales):
     rows = scales[0].bitcast(I32)
     for r in range(4):
-        nc.sync.dma_start(out=plane[r:P:32, :], in_=rows[r:16:4, :])
+        queues[r % len(queues)].dma_start(out=plane[r:P:32, :], in_=rows[r:16:4, :])
 
 
 def tile_list_engram_hl_add_kernel(
@@ -38,7 +39,6 @@ def tile_list_engram_hl_add_kernel(
     nc = tc.nc
     with ExitStack() as ctx:
         keep = ctx.enter_context(tc.tile_pool(name="keep", bufs=1))
-        ring = ctx.enter_context(tc.tile_pool(name="ring", bufs=4))
         keys = ctx.enter_context(tc.psum_pool(name="keys", bufs=3))
         vals = ctx.enter_context(tc.psum_pool(name="vals", bufs=5))
 
@@ -47,19 +47,19 @@ def tile_list_engram_hl_add_kernel(
         table_sc = keep.tile([P, T // 4], I32, name="table_sc", align_bytes=64)
         wk_codes = keep.tile([P, N // 2], I32, name="wk_codes", align_bytes=64)
         wk_sc = keep.tile([P, N // 4], I32, name="wk_sc", align_bytes=64)
-        nc.vector.memset(table_sc[:], 0)
-        nc.gpsimd.memset(wk_sc[:], 0)
+        nc.gpsimd.memset(table_sc[:, : T // 8], 0)
+        nc.vector.memset(table_sc[:, T // 8 :], 0)
+        nc.vector.memset(wk_sc[:], 0)
 
         wv_rows = wv.rearrange("(p i) n -> p i n", i=PACK)
-        wv_raw = [keep.tile([P, PACK, w], F32, name="wv_raw%d" % h) for h, (n0, w) in enumerate(LOADS)]
+        wv_raw = [keep.tile([P, PACK, w], F32, name="wv_raw%d" % h, tag="wv_raw%d" % h, align_bytes=64) for h, (n0, w) in enumerate(LOADS)]
         nc.sync.dma_start(offsets[:], offs)
-        nc.sync.dma_start(out=wk_codes[:], in_=wk_words[0].bitcast(I32))
-        load_scale_rows(nc, table_sc, tab_scales)
+        load_scale_rows((nc.sync, nc.scalar), table_sc, tab_scales)
         nc.sync.dma_start(out=table[:], in_=tab_words[0].rearrange("p t i -> p (t i)").bitcast(I32))
-        nc.sync.dma_start(out=wv_raw[0][:], in_=wv_rows[:, :, 0:256])
-        nc.sync.dma_start(out=wv_raw[1][:], in_=wv_rows[:, :, 256:512])
-        nc.sync.dma_start(out=wv_raw[2][:], in_=wv_rows[:, :, 512:])
-        load_scale_rows(nc, wk_sc, wk_scales)
+        for h, (n0, w) in enumerate(LOADS):
+            nc.sync.dma_start(out=wv_raw[h][:], in_=wv_rows[:, :, n0 : n0 + w])
+        load_scale_rows((nc.sync,), wk_sc, wk_scales)
+        nc.sync.dma_start(out=wk_codes[:], in_=wk_words[0].bitcast(I32))
         st_sb, res_sb = [], []
         for pair in range(N_TILES // 2):
             rows = slice(2 * P * pair, 2 * P * (pair + 1))
@@ -78,7 +78,7 @@ def tile_list_engram_hl_add_kernel(
 
         raws, tops, parts, codes, planes = [], [], {}, [], []
         for c, (n0, width) in enumerate(CHUNKS):
-            h = min(c, 2)
+            h = max(k for k, (l0, w) in enumerate(LOADS) if l0 <= n0)
             c0 = n0 - LOADS[h][0]
             raws.append(wv_raw[h][:, :, c0 : c0 + width])
             top = keep.tile([P, width * PACK], BF16, name="top%d" % c, align_bytes=64)
@@ -88,33 +88,40 @@ def tile_list_engram_hl_add_kernel(
                 in_=upper.rearrange("p i (c u) -> p c i u", u=2),
             )
             tops.append(top)
-            codes.append(keep.tile([P, 2 * width], U32, name="codes%d" % c, align_bytes=64))
+            if c < len(CHUNKS) - 1:
+                parts[c] = keep.tile([P, 2 * width * PACK], BF16, name="parts%d" % c, align_bytes=64)
+                codes.append(keep.tile([P, 2 * width], U32, name="codes%d" % c, align_bytes=64))
             planes.append(keep.tile([P, 2 * width], U8, name="plane%d" % c, align_bytes=64))
 
+        woven = keep.tile([P, CHUNKS[-1][1] * PACK], F32, name="woven")
+        nc.scalar.copy(
+            out=woven[:].rearrange("p (c u i) -> p c i u", u=2, i=PACK),
+            in_=raws[-1].rearrange("p i (c u) -> p c i u", u=2),
+        )
+
         def mask(c):
-            width = CHUNKS[c][1]
-            parts[c] = keep.tile([P, 2, width * PACK], BF16, name="parts%d" % c, align_bytes=64)
             nc.vector.tensor_scalar(
-                out=parts[c][:, 0, :].bitcast(I32), in0=tops[c][:].bitcast(I32),
+                out=parts[c][:, : PACK * CHUNKS[c][1]].bitcast(I32), in0=tops[c][:].bitcast(I32),
                 scalar1=KEEP_TWO_HI, scalar2=None, op0=ALU.bitwise_and,
             )
 
         def rest(c):
+            span = PACK * CHUNKS[c][1]
             nc.vector.tensor_tensor(
-                out=parts[c][:, 1, :].rearrange("p (c u i) -> p c i u", u=2, i=PACK),
+                out=parts[c][:, span:].rearrange("p (c u i) -> p c i u", u=2, i=PACK),
                 in0=raws[c].rearrange("p i (c u) -> p c i u", u=2),
-                in1=parts[c][:, 0, :].rearrange("p (c u i) -> p c i u", u=2, i=PACK),
+                in1=parts[c][:, :span].rearrange("p (c u i) -> p c i u", u=2, i=PACK),
                 op=ALU.subtract,
             )
 
         def quantize(c):
             nc.vector.quantize_mx(
                 out=codes[c][:].bitcast(FP8X4), scales=planes[c][:],
-                in_=parts[c][:].rearrange("p s x -> p (s x)"),
+                in_=parts[c][:],
             )
 
         units = [(nt, jh) for nt in range(N_TILES) for jh in range(J // BANK)]
-        gates, values, gated = {}, {}, {}
+        values = {}
 
         def front(u):
             nt, jh = units[u]
@@ -138,26 +145,23 @@ def tile_list_engram_hl_add_kernel(
                     lhsT=codes[c][:, cols].bitcast(FP8X4), lhsT_scale=planes[c][:, cols],
                     rhs=rhs, rhs_scale=rhs_sc, start=(part == 0), stop=(part == 1),
                 )
-            logit = ring.tile([P, BANK], F32, name="logit")
-            nc.vector.tensor_tensor(out=logit[:], in0=key[:], in1=st_sb[nt][:, js], op=ALU.add)
-            gate = ring.tile([P, BANK], F32, name="gate")
-            nc.scalar.activation(out=gate[:], in_=logit[:], func=ACT.Sigmoid)
-            gates[u], values[u] = gate, value
+            held = st_sb[nt][:, js]
+            logit = keep.tile([P, BANK], F32, name="logit", tag="first", align_bytes=64)[:] if u == 0 else held
+            nc.vector.tensor_tensor(out=logit, in0=key[:], in1=held, op=ALU.add)
+            nc.scalar.activation(out=held, in_=logit, func=ACT.Sigmoid)
+            values[u] = value
 
         def back(u):
             nt, jh = units[u]
-            if jh == 0:
-                gated[nt] = ring.tile([P, J], F32, name="gated")
             js = slice(jh * BANK, (jh + 1) * BANK)
-            nc.vector.tensor_tensor(out=gated[nt][:, js], in0=values[u][:], in1=gates[u][:], op=ALU.mult)
+            nc.vector.tensor_tensor(out=st_sb[nt][:, js], in0=values[u][:], in1=st_sb[nt][:, js], op=ALU.mult)
 
-        results = [keep.tile([P, J], F32, name="result%d" % nt) for nt in range(N_TILES)]
 
         def add_res(nt, js, engine):
-            engine.tensor_tensor(out=results[nt][:, js], in0=gated[nt][:, js], in1=res_sb[nt][:, js], op=ALU.add)
+            engine.tensor_tensor(out=res_sb[nt][:, js], in0=st_sb[nt][:, js], in1=res_sb[nt][:, js], op=ALU.add)
 
         def store(nt, js):
-            nc.sync.dma_start(out=out[nt * P : (nt + 1) * P, js], in_=results[nt][:, js])
+            nc.sync.dma_start(out=out[nt * P : (nt + 1) * P, js], in_=res_sb[nt][:, js])
 
         nc.vector.tensor_copy(picked_sc[:], table_sc[:].bitcast(U8).indirect(offsets[:]))
         nc.vector.tensor_copy(picked[:], table[:].bitcast(U32).indirect(offsets[:]))
@@ -168,37 +172,41 @@ def tile_list_engram_hl_add_kernel(
         rest(1)
         mask(2)
         quantize(1)
-        rest(2)
         mask(3)
-        quantize(2)
+        rest(2)
         rest(3)
-        front(0)
+        quantize(2)
+        span = PACK * CHUNKS[4][1]
+        parts[4] = keep.tile([P, 2 * span], BF16, name="parts4", tag="wv_raw2", align_bytes=64)
+        mask(4)
+        nc.gpsimd.tensor_tensor(out=parts[4][:, span:], in0=woven[:], in1=parts[4][:, :span], op=ALU.subtract)
         quantize(3)
+        for u in range(3):
+            front(u)
+        codes.append(keep.tile([P, 2 * CHUNKS[4][1]], U32, name="codes4", tag="first", align_bytes=64))
+        quantize(4)
 
         halves = (slice(0, BANK), slice(BANK, J))
         whole = slice(0, J)
         last = len(units) - 1
-        back(0)
-        add_res(0, halves[0], nc.gpsimd)
-        front(1)
-        front(2)
         ahead = 3
-        for u in range(1, last + 1):
+        for u in range(last + 1):
             back(u)
             nt, jh = units[u]
-            if u == 1:
-                add_res(0, halves[1], nc.gpsimd)
-                store(0, whole)
+            if nt == 0:
+                add_res(0, halves[jh], nc.gpsimd)
             elif u == last - 3:
-                add_res(nt, halves[0], nc.gpsimd)
-                store(nt, halves[0])
+                add_res(nt, slice(0, LAST_PIECE), nc.gpsimd)
             elif u < last - 3 and jh == 1:
                 add_res(nt, whole, nc.gpsimd)
+            if u < last - 3 and jh == 1:
                 store(nt, whole)
             lead = 2 if u < last - 4 else 3
             while ahead <= min(u + lead, last):
                 front(ahead)
                 ahead += 1
+        add_res(N_TILES - 2, slice(LAST_PIECE, BANK), nc.vector)
+        store(N_TILES - 2, halves[0])
         for nt, jh in units[last - 2 :]:
             add_res(nt, halves[jh], nc.vector)
             store(nt, halves[jh])

@@ -20,10 +20,11 @@ P = 128
 PACK = 4
 BANK = 512
 N_TILES = N // P
-HALF = N // 2
-CHUNKS = ((0, 256), (256, 256), (512, 256), (768, 128), (896, 128))
-LOADS = ((0, 256), (256, 256), (512, 384), (896, 128))
-LAST_PIECE = 128
+QUARTER = N // 4
+SPAN = PACK * QUARTER
+RES_LOADS = ((0, 1), (1, 2), (3, 2), (5, 3))
+LAST_PIECE = 384
+LEAD = 2
 KEEP_TWO_HI = 0xFFF0FFF0 - (1 << 32)
 
 
@@ -33,14 +34,23 @@ def load_scale_rows(queues, plane, scales):
         queues[r % len(queues)].dma_start(out=plane[r:P:32, :], in_=rows[r:16:4, :])
 
 
+def in_word_order(ap):
+    return ap.rearrange("p (c u i) -> p c i u", u=2, i=PACK)
+
+
+def by_pairs(ap):
+    return ap.rearrange("p i (c u) -> p c i u", u=2)
+
+
 def tile_list_engram_hl_add_kernel(
     tc, tab_words, tab_scales, wk_words, wk_scales, wv, st, res, offs, out
 ):
     nc = tc.nc
     with ExitStack() as ctx:
         keep = ctx.enter_context(tc.tile_pool(name="keep", bufs=1))
-        keys = ctx.enter_context(tc.psum_pool(name="keys", bufs=3))
-        vals = ctx.enter_context(tc.psum_pool(name="vals", bufs=5))
+        shared = ctx.enter_context(tc.tile_pool(name="shared", bufs=1))
+        keys = ctx.enter_context(tc.psum_pool(name="keys", bufs=4))
+        vals = ctx.enter_context(tc.psum_pool(name="vals", bufs=4))
 
         offsets = keep.tile([P, J // 16], U16, name="offsets")
         table = keep.tile([P, T], I32, name="table", align_bytes=64)
@@ -52,161 +62,184 @@ def tile_list_engram_hl_add_kernel(
         nc.vector.memset(wk_sc[:], 0)
 
         wv_rows = wv.rearrange("(p i) n -> p i n", i=PACK)
-        wv_raw = [keep.tile([P, PACK, w], F32, name="wv_raw%d" % h, tag="wv_raw%d" % h, align_bytes=64) for h, (n0, w) in enumerate(LOADS)]
+        wv_raw = [keep.tile([P, PACK, QUARTER], F32, name="wv_raw%d" % q, tag="wv_raw%d" % q, align_bytes=64) for q in range(4)]
         nc.sync.dma_start(offsets[:], offs)
         load_scale_rows((nc.sync, nc.scalar), table_sc, tab_scales)
-        nc.sync.dma_start(out=table[:], in_=tab_words[0].rearrange("p t i -> p (t i)").bitcast(I32))
-        for h, (n0, w) in enumerate(LOADS):
-            nc.sync.dma_start(out=wv_raw[h][:], in_=wv_rows[:, :, n0 : n0 + w])
+        for q in range(4):
+            nc.sync.dma_start(out=wv_raw[q][:], in_=wv_rows[:, :, q * QUARTER : (q + 1) * QUARTER])
         load_scale_rows((nc.sync,), wk_sc, wk_scales)
         nc.sync.dma_start(out=wk_codes[:], in_=wk_words[0].bitcast(I32))
-        st_sb, res_sb = [], []
+        nc.sync.dma_start(out=table[:], in_=tab_words[0].rearrange("p t i -> p (t i)").bitcast(I32))
+        st_sb, res_sb, res_tiles = [], [], []
         for pair in range(N_TILES // 2):
-            rows = slice(2 * P * pair, 2 * P * (pair + 1))
             st_pair = keep.tile([P, 2, J], F32, name="st%d" % pair)
-            res_pair = keep.tile([P, 2, J], F32, name="res%d" % pair)
+            rows = slice(2 * P * pair, 2 * P * (pair + 1))
             nc.sync.dma_start(out=st_pair[:], in_=st[rows, :].rearrange("(r p) j -> p r j", p=P))
-            if pair > 0:
-                nc.sync.dma_start(out=behind[0][:], in_=behind[1])
-            behind = (res_pair, res[rows, :].rearrange("(r p) j -> p r j", p=P))
             st_sb.extend([st_pair[:, 0, :], st_pair[:, 1, :]])
-            res_sb.extend([res_pair[:, 0, :], res_pair[:, 1, :]])
-        nc.sync.dma_start(out=behind[0][:], in_=behind[1])
+            first, count = RES_LOADS[pair]
+            res_run = keep.tile([P, count, J], F32, name="res%d" % pair)
+            rows = slice(P * first, P * (first + count))
+            nc.sync.dma_start(out=res_run[:], in_=res[rows, :].rearrange("(r p) j -> p r j", p=P))
+            res_sb.extend([res_run[:, r, :] for r in range(count)])
+            res_tiles.append(res_run)
 
-        picked = keep.tile([P, J], U32, name="picked", align_bytes=64)
         picked_sc = keep.tile([P, J], U8, name="picked_sc", align_bytes=64)
+        nc.vector.tensor_copy(picked_sc[:], table_sc[:].bitcast(U8).indirect(offsets[:]))
 
-        raws, tops, parts, codes, planes = [], [], {}, [], []
-        for c, (n0, width) in enumerate(CHUNKS):
-            h = max(k for k, (l0, w) in enumerate(LOADS) if l0 <= n0)
-            c0 = n0 - LOADS[h][0]
-            raws.append(wv_raw[h][:, :, c0 : c0 + width])
-            top = keep.tile([P, width * PACK], BF16, name="top%d" % c, align_bytes=64)
-            upper = wv_raw[h][:].bitcast(BF16)[:, :, 2 * c0 + 1 : 2 * (c0 + width) : 2]
-            nc.scalar.copy(
-                out=top[:].rearrange("p (c u i) -> p c i u", u=2, i=PACK),
-                in_=upper.rearrange("p i (c u) -> p c i u", u=2),
-            )
-            tops.append(top)
-            if c < len(CHUNKS) - 1:
-                parts[c] = keep.tile([P, 2 * width * PACK], BF16, name="parts%d" % c, align_bytes=64)
-                codes.append(keep.tile([P, 2 * width], U32, name="codes%d" % c, align_bytes=64))
-            planes.append(keep.tile([P, 2 * width], U8, name="plane%d" % c, align_bytes=64))
+        tops = [keep.tile([P, SPAN], BF16, name="top%d" % q, align_bytes=64) for q in range(2)]
+        top_late = shared.tile([P, 2 * SPAN], BF16, name="top_late", align_bytes=64, offset=0)
+        top_of = [tops[0][:], tops[1][:], top_late[:, :SPAN], top_late[:, SPAN:]]
+        for q in range(4):
+            nc.scalar.copy(out=in_word_order(top_of[q]), in_=by_pairs(wv_raw[q][:].bitcast(BF16)[:, :, 1 : 2 * QUARTER : 2]))
+        woven = [keep.tile([P, SPAN], F32, name="woven%d" % q) for q in range(2)]
+        for q in range(2):
+            nc.scalar.copy(out=in_word_order(woven[q][:]), in_=by_pairs(wv_raw[2 + q][:]))
+        warm = keep.tile([P, 8], F32, name="warm")
+        nc.scalar.activation(out=warm[:, 0:1], in_=woven[1][:, 0:1], func=ACT.Sigmoid)
 
-        woven = keep.tile([P, CHUNKS[-1][1] * PACK], F32, name="woven")
-        nc.scalar.copy(
-            out=woven[:].rearrange("p (c u i) -> p c i u", u=2, i=PACK),
-            in_=raws[-1].rearrange("p i (c u) -> p c i u", u=2),
-        )
+        parts = [
+            shared.tile([P, 2 * SPAN], BF16, name="parts0", align_bytes=64, offset=4 * SPAN),
+            keep.tile([P, 2 * SPAN], BF16, name="parts1", align_bytes=64),
+        ]
+        widths = (QUARTER, QUARTER, 2 * QUARTER)
+        codes = [keep.tile([P, 2 * w], U32, name="codes%d" % c, align_bytes=64) for c, w in enumerate(widths[:2])]
+        planes = [keep.tile([P, 2 * w], U8, name="plane%d" % c, align_bytes=64) for c, w in enumerate(widths)]
 
-        def mask(c):
+        def mask(c, top, c0, w):
+            cols = slice(PACK * c0, PACK * (c0 + w))
             nc.vector.tensor_scalar(
-                out=parts[c][:, : PACK * CHUNKS[c][1]].bitcast(I32), in0=tops[c][:].bitcast(I32),
+                out=parts[c][:, cols].bitcast(I32), in0=top[:, cols].bitcast(I32),
                 scalar1=KEEP_TWO_HI, scalar2=None, op0=ALU.bitwise_and,
             )
 
-        def rest(c):
-            span = PACK * CHUNKS[c][1]
+        def rest(q, c0, w):
             nc.vector.tensor_tensor(
-                out=parts[c][:, span:].rearrange("p (c u i) -> p c i u", u=2, i=PACK),
-                in0=raws[c].rearrange("p i (c u) -> p c i u", u=2),
-                in1=parts[c][:, :span].rearrange("p (c u i) -> p c i u", u=2, i=PACK),
-                op=ALU.subtract,
+                out=in_word_order(parts[q][:, SPAN + PACK * c0 : SPAN + PACK * (c0 + w)]),
+                in0=by_pairs(wv_raw[q][:, :, c0 : c0 + w]),
+                in1=in_word_order(parts[q][:, PACK * c0 : PACK * (c0 + w)]), op=ALU.subtract,
             )
 
         def quantize(c):
-            nc.vector.quantize_mx(
-                out=codes[c][:].bitcast(FP8X4), scales=planes[c][:],
-                in_=parts[c][:],
+            nc.vector.quantize_mx(out=codes[c][:].bitcast(FP8X4), scales=planes[c][:], in_=parts[c][:])
+
+        mask(0, tops[0], 0, P)
+        mask(0, tops[0], P, P)
+        rest(0, 0, P)
+        rest(0, P, P)
+        mask(1, tops[1], 0, QUARTER)
+        quantize(0)
+        rest(1, 0, QUARTER)
+        parts.append(shared.tile([P, 4 * SPAN], BF16, name="parts2", align_bytes=64, offset=4 * SPAN))
+        mask(2, top_late, 0, 2 * QUARTER)
+        for q in range(2):
+            nc.gpsimd.tensor_tensor(
+                out=parts[2][:, (2 + q) * SPAN : (3 + q) * SPAN], in0=woven[q][:],
+                in1=parts[2][:, q * SPAN : (q + 1) * SPAN], op=ALU.subtract,
+            )
+        quantize(1)
+        picked = [shared.tile([P, BANK], U32, name="picked%d" % jh, align_bytes=64, offset=4 * BANK * jh) for jh in range(J // BANK)]
+        for jh in range(J // BANK):
+            nc.vector.tensor_copy(
+                picked[jh][:],
+                table[:].bitcast(U32).indirect(offsets[:, jh * BANK // 16 : (jh + 1) * BANK // 16]),
             )
 
         units = [(nt, jh) for nt in range(N_TILES) for jh in range(J // BANK)]
         values = {}
+        gated = list(st_sb)
+        result = list(res_sb)
 
-        def front(u):
+        def gate(u, logit=None):
             nt, jh = units[u]
             js = slice(jh * BANK, (jh + 1) * BANK)
-            rhs = picked[:, js].bitcast(FP8X4)
-            rhs_sc = picked_sc[:, js]
             key = keys.tile([P, BANK], F32, name="key")
             nc.tensor.matmul_mx(
                 out=key[:],
                 lhsT=wk_codes[:].bitcast(U8)[:, 2 * P * nt : 2 * P * (nt + 1)].bitcast(FP4X4),
                 lhsT_scale=wk_sc[:].bitcast(U8)[:, P * nt : P * (nt + 1)],
-                rhs=rhs, rhs_scale=rhs_sc, start=True, stop=True,
+                rhs=picked[jh][:].bitcast(FP8X4), rhs_scale=picked_sc[:, js], start=True, stop=True,
             )
-            value = vals.tile([P, BANK], F32, name="value")
-            c = max(k for k, (n0, width) in enumerate(CHUNKS) if n0 <= nt * P)
-            n0, width = CHUNKS[c]
-            for part in range(2):
-                cols = slice(part * width + nt * P - n0, part * width + nt * P - n0 + P)
-                nc.tensor.matmul_mx(
-                    out=value[:],
-                    lhsT=codes[c][:, cols].bitcast(FP8X4), lhsT_scale=planes[c][:, cols],
-                    rhs=rhs, rhs_scale=rhs_sc, start=(part == 0), stop=(part == 1),
-                )
             held = st_sb[nt][:, js]
-            logit = keep.tile([P, BANK], F32, name="logit", tag="first", align_bytes=64)[:] if u == 0 else held
+            logit = held if logit is None else logit
             nc.vector.tensor_tensor(out=logit, in0=key[:], in1=held, op=ALU.add)
             nc.scalar.activation(out=held, in_=logit, func=ACT.Sigmoid)
+
+        def product(u):
+            nt, jh = units[u]
+            js = slice(jh * BANK, (jh + 1) * BANK)
+            value = vals.tile([P, BANK], F32, name="value")
+            c = min(nt * P // QUARTER, 2)
+            for part in range(2):
+                first = part * widths[c] + nt * P - c * QUARTER
+                nc.tensor.matmul_mx(
+                    out=value[:],
+                    lhsT=codes[c][:, first : first + P].bitcast(FP8X4), lhsT_scale=planes[c][:, first : first + P],
+                    rhs=picked[jh][:].bitcast(FP8X4), rhs_scale=picked_sc[:, js], start=(part == 0), stop=(part == 1),
+                )
             values[u] = value
+
+        def front(u, logit=None):
+            gate(u, logit)
+            product(u)
 
         def back(u):
             nt, jh = units[u]
             js = slice(jh * BANK, (jh + 1) * BANK)
-            nc.vector.tensor_tensor(out=st_sb[nt][:, js], in0=values[u][:], in1=st_sb[nt][:, js], op=ALU.mult)
-
+            nc.vector.tensor_tensor(out=gated[nt][:, js], in0=values[u][:], in1=st_sb[nt][:, js], op=ALU.mult)
 
         def add_res(nt, js, engine):
-            engine.tensor_tensor(out=res_sb[nt][:, js], in0=st_sb[nt][:, js], in1=res_sb[nt][:, js], op=ALU.add)
+            engine.tensor_tensor(out=result[nt][:, js], in0=gated[nt][:, js], in1=res_sb[nt][:, js], op=ALU.add)
 
         def store(nt, js):
-            nc.sync.dma_start(out=out[nt * P : (nt + 1) * P, js], in_=res_sb[nt][:, js])
+            nc.sync.dma_start(out=out[nt * P : (nt + 1) * P, js], in_=result[nt][:, js])
 
-        nc.vector.tensor_copy(picked_sc[:], table_sc[:].bitcast(U8).indirect(offsets[:]))
-        nc.vector.tensor_copy(picked[:], table[:].bitcast(U32).indirect(offsets[:]))
-        mask(0)
-        rest(0)
-        mask(1)
-        quantize(0)
-        rest(1)
-        mask(2)
-        quantize(1)
-        mask(3)
-        rest(2)
-        rest(3)
-        quantize(2)
-        span = PACK * CHUNKS[4][1]
-        parts[4] = keep.tile([P, 2 * span], BF16, name="parts4", tag="wv_raw2", align_bytes=64)
-        mask(4)
-        nc.gpsimd.tensor_tensor(out=parts[4][:, span:], in0=woven[:], in1=parts[4][:, :span], op=ALU.subtract)
-        quantize(3)
-        for u in range(3):
-            front(u)
-        codes.append(keep.tile([P, 2 * CHUNKS[4][1]], U32, name="codes4", tag="first", align_bytes=64))
-        quantize(4)
+        def store_pair(run):
+            first = RES_LOADS[run][0]
+            nc.sync.dma_start(
+                out=out[first * P : (first + 2) * P, :].rearrange("(r p) j -> p r j", p=P), in_=res_tiles[run][:]
+            )
 
         halves = (slice(0, BANK), slice(BANK, J))
         whole = slice(0, J)
+        first_logit = keep.tile([P, BANK], F32, name="first_logit", tag="first", align_bytes=64)
+        gate(0, first_logit[:])
+        gate(2)
+        gate(1)
+        product(0)
+        back(0)
+        codes.append(keep.tile([P, 2 * widths[2]], U32, name="codes2", tag="first", align_bytes=64))
+        quantize(2)
+        after = shared.tile([P, 2 * J + BANK], F32, name="after", align_bytes=64, offset=4 * SPAN)
+        result[0] = after[:, :J]
+        gated[1] = after[:, J : 2 * J]
+        add_res(0, halves[0], nc.gpsimd)
+        gate(3)
+        for u in (1, 2, 3):
+            product(u)
+        back(1)
+        add_res(0, halves[1], nc.gpsimd)
+        store(0, whole)
+        front(4, after[:, 2 * J :])
+
         last = len(units) - 1
-        ahead = 3
-        for u in range(last + 1):
+        ahead = 5
+        for u in range(2, last + 1):
+            while ahead <= min(u + LEAD, last):
+                front(ahead)
+                ahead += 1
             back(u)
             nt, jh = units[u]
-            if nt == 0:
-                add_res(0, halves[jh], nc.gpsimd)
-            elif u == last - 3:
+            if u == last - 3:
                 add_res(nt, slice(0, LAST_PIECE), nc.gpsimd)
             elif u < last - 3 and jh == 1:
                 add_res(nt, whole, nc.gpsimd)
-            if u < last - 3 and jh == 1:
-                store(nt, whole)
-            lead = 2 if u < last - 4 else 3
-            while ahead <= min(u + lead, last):
-                front(ahead)
-                ahead += 1
+                if nt in (2, 4):
+                    store_pair(nt // 2)
+                elif nt == 5:
+                    store(nt, whole)
         add_res(N_TILES - 2, slice(LAST_PIECE, BANK), nc.vector)
-        store(N_TILES - 2, halves[0])
-        for nt, jh in units[last - 2 :]:
-            add_res(nt, halves[jh], nc.vector)
-            store(nt, halves[jh])
+        add_res(N_TILES - 2, halves[1], nc.vector)
+        store(N_TILES - 2, whole)
+        for jh in range(2):
+            add_res(N_TILES - 1, halves[jh], nc.vector)
+            store(N_TILES - 1, halves[jh])

@@ -23,7 +23,6 @@ N_TILES = N // P
 QUARTER = N // 4
 SPAN = PACK * QUARTER
 RES_LOADS = ((0, 1), (1, 2), (3, 2), (5, 3))
-LAST_PIECE = 384
 LEAD = 2
 KEEP_TWO_HI = 0xFFF0FFF0 - (1 << 32)
 
@@ -94,8 +93,6 @@ def tile_list_engram_hl_add_kernel(
         woven = [keep.tile([P, SPAN], F32, name="woven%d" % q) for q in range(2)]
         for q in range(2):
             nc.scalar.copy(out=in_word_order(woven[q][:]), in_=by_pairs(wv_raw[2 + q][:]))
-        warm = keep.tile([P, 8], F32, name="warm")
-        nc.scalar.activation(out=warm[:, 0:1], in_=woven[1][:, 0:1], func=ACT.Sigmoid)
 
         parts = [
             shared.tile([P, 2 * SPAN], BF16, name="parts0", align_bytes=64, offset=4 * SPAN),
@@ -146,10 +143,12 @@ def tile_list_engram_hl_add_kernel(
 
         units = [(nt, jh) for nt in range(N_TILES) for jh in range(J // BANK)]
         values = {}
-        gated = list(st_sb)
+        gates = [st_sb[nt][:, jh * BANK : (jh + 1) * BANK] for nt, jh in units]
+        first_gate = keep.tile([P, BANK], F32, name="first_gate", tag="first", align_bytes=64)
+        gates[0] = first_gate[:]
         result = list(res_sb)
 
-        def gate(u, logit=None):
+        def gate(u):
             nt, jh = units[u]
             js = slice(jh * BANK, (jh + 1) * BANK)
             key = keys.tile([P, BANK], F32, name="key")
@@ -159,10 +158,8 @@ def tile_list_engram_hl_add_kernel(
                 lhsT_scale=wk_sc[:].bitcast(U8)[:, P * nt : P * (nt + 1)],
                 rhs=picked[jh][:].bitcast(FP8X4), rhs_scale=picked_sc[:, js], start=True, stop=True,
             )
-            held = st_sb[nt][:, js]
-            logit = held if logit is None else logit
-            nc.vector.tensor_tensor(out=logit, in0=key[:], in1=held, op=ALU.add)
-            nc.scalar.activation(out=held, in_=logit, func=ACT.Sigmoid)
+            nc.vector.tensor_tensor(out=gates[u], in0=key[:], in1=st_sb[nt][:, js], op=ALU.add)
+            nc.scalar.activation(out=gates[u], in_=gates[u], func=ACT.Sigmoid)
 
         def product(u):
             nt, jh = units[u]
@@ -178,17 +175,17 @@ def tile_list_engram_hl_add_kernel(
                 )
             values[u] = value
 
-        def front(u, logit=None):
-            gate(u, logit)
+        def front(u):
+            gate(u)
             product(u)
 
         def back(u):
             nt, jh = units[u]
             js = slice(jh * BANK, (jh + 1) * BANK)
-            nc.vector.tensor_tensor(out=gated[nt][:, js], in0=values[u][:], in1=st_sb[nt][:, js], op=ALU.mult)
+            nc.vector.tensor_tensor(out=st_sb[nt][:, js], in0=values[u][:], in1=gates[u], op=ALU.mult)
 
         def add_res(nt, js, engine):
-            engine.tensor_tensor(out=result[nt][:, js], in0=gated[nt][:, js], in1=res_sb[nt][:, js], op=ALU.add)
+            engine.tensor_tensor(out=result[nt][:, js], in0=st_sb[nt][:, js], in1=res_sb[nt][:, js], op=ALU.add)
 
         def store(nt, js):
             nc.sync.dma_start(out=out[nt * P : (nt + 1) * P, js], in_=result[nt][:, js])
@@ -201,45 +198,35 @@ def tile_list_engram_hl_add_kernel(
 
         halves = (slice(0, BANK), slice(BANK, J))
         whole = slice(0, J)
-        first_logit = keep.tile([P, BANK], F32, name="first_logit", tag="first", align_bytes=64)
-        gate(0, first_logit[:])
-        gate(2)
-        gate(1)
+        for u in (0, 2, 1):
+            gate(u)
         product(0)
         back(0)
-        codes.append(keep.tile([P, 2 * widths[2]], U32, name="codes2", tag="first", align_bytes=64))
-        quantize(2)
-        after = shared.tile([P, 2 * J + BANK], F32, name="after", align_bytes=64, offset=4 * SPAN)
-        result[0] = after[:, :J]
-        gated[1] = after[:, J : 2 * J]
-        add_res(0, halves[0], nc.gpsimd)
         gate(3)
         for u in (1, 2, 3):
             product(u)
         back(1)
-        add_res(0, halves[1], nc.gpsimd)
+        codes.append(keep.tile([P, 2 * widths[2]], U32, name="codes2", tag="first", align_bytes=64))
+        quantize(2)
+        after = shared.tile([P, J], F32, name="after", align_bytes=64, offset=4 * SPAN)
+        result[0] = after[:]
+        add_res(0, whole, nc.gpsimd)
         store(0, whole)
-        front(4, after[:, 2 * J :])
 
         last = len(units) - 1
-        ahead = 5
+        ahead = 4
         for u in range(2, last + 1):
             while ahead <= min(u + LEAD, last):
                 front(ahead)
                 ahead += 1
             back(u)
             nt, jh = units[u]
-            if u == last - 3:
-                add_res(nt, slice(0, LAST_PIECE), nc.gpsimd)
-            elif u < last - 3 and jh == 1:
+            if u < last - 3 and jh == 1:
                 add_res(nt, whole, nc.gpsimd)
                 if nt in (2, 4):
                     store_pair(nt // 2)
                 elif nt == 5:
                     store(nt, whole)
-        add_res(N_TILES - 2, slice(LAST_PIECE, BANK), nc.vector)
-        add_res(N_TILES - 2, halves[1], nc.vector)
-        store(N_TILES - 2, whole)
-        for jh in range(2):
-            add_res(N_TILES - 1, halves[jh], nc.vector)
-            store(N_TILES - 1, halves[jh])
+        for nt, jh in units[last - 3 :]:
+            add_res(nt, halves[jh], nc.vector)
+            store(nt, halves[jh])

@@ -63,11 +63,11 @@ def tile_list_engram_hl_add_kernel(
         wv_rows = wv.rearrange("(p i) n -> p i n", i=PACK)
         wv_raw = [keep.tile([P, PACK, QUARTER], F32, name="wv_raw%d" % q, tag="wv_raw%d" % q, align_bytes=64) for q in range(4)]
         nc.sync.dma_start(offsets[:], offs)
+        nc.sync.dma_start(out=wk_codes[:], in_=wk_words[0].bitcast(I32))
         load_scale_rows((nc.sync, nc.scalar), table_sc, tab_scales)
         for q in range(4):
             nc.sync.dma_start(out=wv_raw[q][:], in_=wv_rows[:, :, q * QUARTER : (q + 1) * QUARTER])
         load_scale_rows((nc.sync,), wk_sc, wk_scales)
-        nc.sync.dma_start(out=wk_codes[:], in_=wk_words[0].bitcast(I32))
         nc.sync.dma_start(out=table[:], in_=tab_words[0].rearrange("p t i -> p (t i)").bitcast(I32))
         st_sb, res_sb, res_tiles = [], [], []
         for pair in range(N_TILES // 2):
@@ -143,9 +143,9 @@ def tile_list_engram_hl_add_kernel(
 
         units = [(nt, jh) for nt in range(N_TILES) for jh in range(J // BANK)]
         values = {}
-        gates = [st_sb[nt][:, jh * BANK : (jh + 1) * BANK] for nt, jh in units]
-        first_gate = keep.tile([P, BANK], F32, name="first_gate", tag="first", align_bytes=64)
-        gates[0] = first_gate[:]
+        logits = [st_sb[nt][:, jh * BANK : (jh + 1) * BANK] for nt, jh in units]
+        first_logit = keep.tile([P, BANK], F32, name="first_logit", tag="first", align_bytes=64)
+        logits[0] = first_logit[:]
         result = list(res_sb)
 
         def gate(u):
@@ -158,8 +158,8 @@ def tile_list_engram_hl_add_kernel(
                 lhsT_scale=wk_sc[:].bitcast(U8)[:, P * nt : P * (nt + 1)],
                 rhs=picked[jh][:].bitcast(FP8X4), rhs_scale=picked_sc[:, js], start=True, stop=True,
             )
-            nc.vector.tensor_tensor(out=gates[u], in0=key[:], in1=st_sb[nt][:, js], op=ALU.add)
-            nc.scalar.activation(out=gates[u], in_=gates[u], func=ACT.Sigmoid)
+            nc.vector.tensor_tensor(out=logits[u], in0=key[:], in1=st_sb[nt][:, js], op=ALU.add)
+            nc.scalar.activation(out=st_sb[nt][:, js], in_=logits[u], func=ACT.Sigmoid)
 
         def product(u):
             nt, jh = units[u]
@@ -182,7 +182,7 @@ def tile_list_engram_hl_add_kernel(
         def back(u):
             nt, jh = units[u]
             js = slice(jh * BANK, (jh + 1) * BANK)
-            nc.vector.tensor_tensor(out=st_sb[nt][:, js], in0=values[u][:], in1=gates[u], op=ALU.mult)
+            nc.vector.tensor_tensor(out=st_sb[nt][:, js], in0=values[u][:], in1=st_sb[nt][:, js], op=ALU.mult)
 
         def add_res(nt, js, engine):
             engine.tensor_tensor(out=result[nt][:, js], in0=st_sb[nt][:, js], in1=res_sb[nt][:, js], op=ALU.add)
@@ -202,21 +202,21 @@ def tile_list_engram_hl_add_kernel(
             gate(u)
         product(0)
         back(0)
-        gate(3)
-        for u in (1, 2, 3):
-            product(u)
-        back(1)
         codes.append(keep.tile([P, 2 * widths[2]], U32, name="codes2", tag="first", align_bytes=64))
         quantize(2)
         after = shared.tile([P, J], F32, name="after", align_bytes=64, offset=4 * SPAN)
         result[0] = after[:]
-        add_res(0, whole, nc.gpsimd)
+        add_res(0, halves[0], nc.gpsimd)
+        product(1)
+        back(1)
+        add_res(0, halves[1], nc.gpsimd)
         store(0, whole)
+        product(2)
 
         last = len(units) - 1
-        ahead = 4
+        ahead = 3
         for u in range(2, last + 1):
-            while ahead <= min(u + LEAD, last):
+            while ahead <= min(u + (1 if u < 6 else LEAD), last):
                 front(ahead)
                 ahead += 1
             back(u)

@@ -34,11 +34,11 @@ def load_scale_rows(queues, plane, scales):
 
 
 def in_word_order(ap):
-    return ap.rearrange("p (c u i) -> p c i u", u=2, i=PACK)
+    return ap.rearrange("p (c u i) -> p c i u", u=4, i=PACK)
 
 
 def by_pairs(ap):
-    return ap.rearrange("p i (c u) -> p c i u", u=2)
+    return ap.rearrange("p i (c u) -> p c i u", u=4)
 
 
 def tile_list_engram_hl_add_kernel(

@@ -1,6 +1,7 @@
 from contextlib import ExitStack
 
 import concourse.mybir as mybir
+from concourse.masks import make_identity
 
 K, N, T, J = 512, 1024, 2048, 1024
 FLOPS = 3 * 2 * K * N * J
@@ -22,7 +23,7 @@ BANK = 512
 N_TILES = N // P
 QUARTER = N // 4
 SPAN = PACK * QUARTER
-RES_LOADS = ((0, 1), (1, 2), (3, 2), (5, 3))
+RES_LOADS = ((0, 1), (1, 2), (3, 3), (6, 2))
 LEAD = 2
 KEEP_TWO_HI = 0xFFF0FFF0 - (1 << 32)
 
@@ -59,6 +60,9 @@ def tile_list_engram_hl_add_kernel(
         nc.gpsimd.memset(table_sc[:, : T // 8], 0)
         nc.vector.memset(table_sc[:, T // 8 :], 0)
         nc.vector.memset(wk_sc[:], 0)
+
+        ident = keep.tile([P, P], F32, name="ident")
+        make_identity(nc, ident[:])
 
         wv_rows = wv.rearrange("(p i) n -> p i n", i=PACK)
         wv_raw = [keep.tile([P, PACK, QUARTER], F32, name="wv_raw%d" % q, tag="wv_raw%d" % q, align_bytes=64) for q in range(4)]
@@ -193,8 +197,25 @@ def tile_list_engram_hl_add_kernel(
         def store_pair(run):
             first = RES_LOADS[run][0]
             nc.sync.dma_start(
-                out=out[first * P : (first + 2) * P, :].rearrange("(r p) j -> p r j", p=P), in_=res_tiles[run][:]
+                out=out[first * P : (first + 2) * P, :].rearrange("(r p) j -> p r j", p=P), in_=res_tiles[run][:, :2, :]
             )
+
+        def add_res_turned(nt, jh):
+            blocks = [slice(jh * BANK + b * P, jh * BANK + (b + 1) * P) for b in range(BANK // P)]
+            turned = keys.tile([P, BANK], F32, name="key")
+            sources = [res_sb[nt][:, cols] for cols in blocks] + [st_sb[nt][:, cols] for cols in blocks]
+            for i, source in enumerate(sources):
+                b = i % len(blocks)
+                nc.tensor.matmul(
+                    turned[:, b * P : (b + 1) * P], source, ident[:], is_transpose=True,
+                    start=(i == 0), stop=(i == len(sources) - 1),
+                )
+            held = keep.tile([P, BANK], F32, name="held")
+            nc.scalar.copy(out=held[:], in_=turned[:])
+            straight = keys.tile([P, BANK], F32, name="key")
+            for b in range(len(blocks)):
+                nc.tensor.transpose(straight[:, b * P : (b + 1) * P], held[:, b * P : (b + 1) * P], ident[:])
+            nc.scalar.copy(out=res_sb[nt][:, jh * BANK : (jh + 1) * BANK], in_=straight[:])
 
         halves = (slice(0, BANK), slice(BANK, J))
         whole = slice(0, J)
@@ -219,14 +240,18 @@ def tile_list_engram_hl_add_kernel(
             while ahead <= min(u + (1 if u < 6 else LEAD), last):
                 front(ahead)
                 ahead += 1
+            if u == 13:
+                add_res_turned(5, 0)
+                store(5, halves[0])
             back(u)
             nt, jh = units[u]
-            if u < last - 3 and jh == 1:
+            if u in (11, 12):
+                add_res(nt, halves[jh], nc.gpsimd)
+                store(nt, halves[jh])
+            elif u < last - 3 and jh == 1:
                 add_res(nt, whole, nc.gpsimd)
                 if nt in (2, 4):
                     store_pair(nt // 2)
-                elif nt == 5:
-                    store(nt, whole)
-        for nt, jh in units[last - 3 :]:
+        for nt, jh in units[last - 2 :]:
             add_res(nt, halves[jh], nc.vector)
             store(nt, halves[jh])

from contextlib import ExitStack

import concourse.mybir as mybir
from concourse.masks import make_identity

K, N, T, J = 512, 1024, 2048, 1024
FLOPS = 3 * 2 * K * N * J

F32 = mybir.dt.float32
BF16 = mybir.dt.bfloat16
I32 = mybir.dt.int32
U32 = mybir.dt.uint32
U16 = mybir.dt.uint16
U8 = mybir.dt.uint8
FP8X4 = mybir.dt.float8_e4m3fn_x4
FP4X4 = mybir.dt.float4_e2m1fn_x4
ALU = mybir.AluOpType
ACT = mybir.ActivationFunctionType

P = 128
PACK = 4
BANK = 512
N_TILES = N // P
QUARTER = N // 4
SPAN = PACK * QUARTER
RES_LOADS = ((0, 1), (1, 2), (3, 3), (6, 2))
LEAD = 2
KEEP_TWO_HI = 0xFFF0FFF0 - (1 << 32)


def load_scale_rows(queues, plane, scales):
    rows = scales[0].bitcast(I32)
    for r in range(4):
        queues[r % len(queues)].dma_start(out=plane[r:P:32, :], in_=rows[r:16:4, :])


def in_word_order(ap):
    return ap.rearrange("p (c u i) -> p c i u", u=4, i=PACK)


def by_pairs(ap):
    return ap.rearrange("p i (c u) -> p c i u", u=4)


def tile_list_engram_hl_add_kernel(
    tc, tab_words, tab_scales, wk_words, wk_scales, wv, st, res, offs, out
):
    nc = tc.nc
    with ExitStack() as ctx:
        keep = ctx.enter_context(tc.tile_pool(name="keep", bufs=1))
        shared = ctx.enter_context(tc.tile_pool(name="shared", bufs=1))
        keys = ctx.enter_context(tc.psum_pool(name="keys", bufs=4))
        vals = ctx.enter_context(tc.psum_pool(name="vals", bufs=4))

        offsets = keep.tile([P, J // 16], U16, name="offsets")
        table = keep.tile([P, T], I32, name="table", align_bytes=64)
        table_sc = keep.tile([P, T // 4], I32, name="table_sc", align_bytes=64)
        wk_codes = keep.tile([P, N // 2], I32, name="wk_codes", align_bytes=64)
        wk_sc = keep.tile([P, N // 4], I32, name="wk_sc", align_bytes=64)
        nc.gpsimd.memset(table_sc[:, : T // 8], 0)
        nc.vector.memset(table_sc[:, T // 8 :], 0)
        nc.vector.memset(wk_sc[:], 0)

        ident = keep.tile([P, P], F32, name="ident")
        make_identity(nc, ident[:])

        wv_rows = wv.rearrange("(p i) n -> p i n", i=PACK)
        wv_raw = [keep.tile([P, PACK, QUARTER], F32, name="wv_raw%d" % q, tag="wv_raw%d" % q, align_bytes=64) for q in range(4)]
        nc.sync.dma_start(offsets[:], offs)
        nc.sync.dma_start(out=wk_codes[:], in_=wk_words[0].bitcast(I32))
        load_scale_rows((nc.sync, nc.scalar), table_sc, tab_scales)
        for q in range(4):
            nc.sync.dma_start(out=wv_raw[q][:], in_=wv_rows[:, :, q * QUARTER : (q + 1) * QUARTER])
        load_scale_rows((nc.sync,), wk_sc, wk_scales)
        nc.sync.dma_start(out=table[:], in_=tab_words[0].rearrange("p t i -> p (t i)").bitcast(I32))
        st_sb, res_sb, res_tiles = [], [], []
        for pair in range(N_TILES // 2):
            st_pair = keep.tile([P, 2, J], F32, name="st%d" % pair)
            rows = slice(2 * P * pair, 2 * P * (pair + 1))
            nc.sync.dma_start(out=st_pair[:], in_=st[rows, :].rearrange("(r p) j -> p r j", p=P))
            st_sb.extend([st_pair[:, 0, :], st_pair[:, 1, :]])
            first, count = RES_LOADS[pair]
            res_run = keep.tile([P, count, J], F32, name="res%d" % pair)
            rows = slice(P * first, P * (first + count))
            nc.sync.dma_start(out=res_run[:], in_=res[rows, :].rearrange("(r p) j -> p r j", p=P))
            res_sb.extend([res_run[:, r, :] for r in range(count)])
            res_tiles.append(res_run)

        picked_sc = keep.tile([P, J], U8, name="picked_sc", align_bytes=64)
        nc.vector.tensor_copy(picked_sc[:], table_sc[:].bitcast(U8).indirect(offsets[:]))

        tops = [keep.tile([P, SPAN], BF16, name="top%d" % q, align_bytes=64) for q in range(2)]
        top_late = shared.tile([P, 2 * SPAN], BF16, name="top_late", align_bytes=64, offset=0)
        top_of = [tops[0][:], tops[1][:], top_late[:, :SPAN], top_late[:, SPAN:]]
        for q in range(4):
            nc.scalar.copy(out=in_word_order(top_of[q]), in_=by_pairs(wv_raw[q][:].bitcast(BF16)[:, :, 1 : 2 * QUARTER : 2]))
        woven = [keep.tile([P, SPAN], F32, name="woven%d" % q) for q in range(2)]
        for q in range(2):
            nc.scalar.copy(out=in_word_order(woven[q][:]), in_=by_pairs(wv_raw[2 + q][:]))

        parts = [
            shared.tile([P, 2 * SPAN], BF16, name="parts0", align_bytes=64, offset=4 * SPAN),
            keep.tile([P, 2 * SPAN], BF16, name="parts1", align_bytes=64),
        ]
        widths = (QUARTER, QUARTER, 2 * QUARTER)
        codes = [keep.tile([P, 2 * w], U32, name="codes%d" % c, align_bytes=64) for c, w in enumerate(widths[:2])]
        planes = [keep.tile([P, 2 * w], U8, name="plane%d" % c, align_bytes=64) for c, w in enumerate(widths)]

        def mask(c, top, c0, w):
            cols = slice(PACK * c0, PACK * (c0 + w))
            nc.vector.tensor_scalar(
                out=parts[c][:, cols].bitcast(I32), in0=top[:, cols].bitcast(I32),
                scalar1=KEEP_TWO_HI, scalar2=None, op0=ALU.bitwise_and,
            )

        def rest(q, c0, w):
            nc.vector.tensor_tensor(
                out=in_word_order(parts[q][:, SPAN + PACK * c0 : SPAN + PACK * (c0 + w)]),
                in0=by_pairs(wv_raw[q][:, :, c0 : c0 + w]),
                in1=in_word_order(parts[q][:, PACK * c0 : PACK * (c0 + w)]), op=ALU.subtract,
            )

        def quantize(c):
            nc.vector.quantize_mx(out=codes[c][:].bitcast(FP8X4), scales=planes[c][:], in_=parts[c][:])

        mask(0, tops[0], 0, P)
        mask(0, tops[0], P, P)
        rest(0, 0, P)
        rest(0, P, P)
        mask(1, tops[1], 0, QUARTER)
        quantize(0)
        rest(1, 0, QUARTER)
        parts.append(shared.tile([P, 4 * SPAN], BF16, name="parts2", align_bytes=64, offset=4 * SPAN))
        mask(2, top_late, 0, 2 * QUARTER)
        for q in range(2):
            nc.gpsimd.tensor_tensor(
                out=parts[2][:, (2 + q) * SPAN : (3 + q) * SPAN], in0=woven[q][:],
                in1=parts[2][:, q * SPAN : (q + 1) * SPAN], op=ALU.subtract,
            )
        quantize(1)
        picked = [shared.tile([P, BANK], U32, name="picked%d" % jh, align_bytes=64, offset=4 * BANK * jh) for jh in range(J // BANK)]
        for jh in range(J // BANK):
            nc.vector.tensor_copy(
                picked[jh][:],
                table[:].bitcast(U32).indirect(offsets[:, jh * BANK // 16 : (jh + 1) * BANK // 16]),
            )

        units = [(nt, jh) for nt in range(N_TILES) for jh in range(J // BANK)]
        values = {}
        logits = [st_sb[nt][:, jh * BANK : (jh + 1) * BANK] for nt, jh in units]
        first_logit = keep.tile([P, BANK], F32, name="first_logit", tag="first", align_bytes=64)
        logits[0] = first_logit[:]
        result = list(res_sb)

        def gate(u):
            nt, jh = units[u]
            js = slice(jh * BANK, (jh + 1) * BANK)
            key = keys.tile([P, BANK], F32, name="key")
            nc.tensor.matmul_mx(
                out=key[:],
                lhsT=wk_codes[:].bitcast(U8)[:, 2 * P * nt : 2 * P * (nt + 1)].bitcast(FP4X4),
                lhsT_scale=wk_sc[:].bitcast(U8)[:, P * nt : P * (nt + 1)],
                rhs=picked[jh][:].bitcast(FP8X4), rhs_scale=picked_sc[:, js], start=True, stop=True,
            )
            nc.vector.tensor_tensor(out=logits[u], in0=key[:], in1=st_sb[nt][:, js], op=ALU.add)
            nc.scalar.activation(out=st_sb[nt][:, js], in_=logits[u], func=ACT.Sigmoid)

        def product(u):
            nt, jh = units[u]
            js = slice(jh * BANK, (jh + 1) * BANK)
            value = vals.tile([P, BANK], F32, name="value")
            c = min(nt * P // QUARTER, 2)
            for part in range(2):
                first = part * widths[c] + nt * P - c * QUARTER
                nc.tensor.matmul_mx(
                    out=value[:],
                    lhsT=codes[c][:, first : first + P].bitcast(FP8X4), lhsT_scale=planes[c][:, first : first + P],
                    rhs=picked[jh][:].bitcast(FP8X4), rhs_scale=picked_sc[:, js], start=(part == 0), stop=(part == 1),
                )
            values[u] = value

        def front(u):
            gate(u)
            product(u)

        def back(u):
            nt, jh = units[u]
            js = slice(jh * BANK, (jh + 1) * BANK)
            nc.vector.tensor_tensor(out=st_sb[nt][:, js], in0=values[u][:], in1=st_sb[nt][:, js], op=ALU.mult)

        def add_res(nt, js, engine):
            engine.tensor_tensor(out=result[nt][:, js], in0=st_sb[nt][:, js], in1=res_sb[nt][:, js], op=ALU.add)

        def store(nt, js):
            nc.sync.dma_start(out=out[nt * P : (nt + 1) * P, js], in_=result[nt][:, js])

        def store_pair(run):
            first = RES_LOADS[run][0]
            nc.sync.dma_start(
                out=out[first * P : (first + 2) * P, :].rearrange("(r p) j -> p r j", p=P), in_=res_tiles[run][:, :2, :]
            )

        def add_res_turned(nt, jh):
            blocks = [slice(jh * BANK + b * P, jh * BANK + (b + 1) * P) for b in range(BANK // P)]
            turned = keys.tile([P, BANK], F32, name="key")
            sources = [res_sb[nt][:, cols] for cols in blocks] + [st_sb[nt][:, cols] for cols in blocks]
            for i, source in enumerate(sources):
                b = i % len(blocks)
                nc.tensor.matmul(
                    turned[:, b * P : (b + 1) * P], source, ident[:], is_transpose=True,
                    start=(i == 0), stop=(i == len(sources) - 1),
                )
            held = keep.tile([P, BANK], F32, name="held")
            nc.scalar.copy(out=held[:], in_=turned[:])
            straight = keys.tile([P, BANK], F32, name="key")
            for b in range(len(blocks)):
                nc.tensor.transpose(straight[:, b * P : (b + 1) * P], held[:, b * P : (b + 1) * P], ident[:])
            nc.scalar.copy(out=res_sb[nt][:, jh * BANK : (jh + 1) * BANK], in_=straight[:])

        halves = (slice(0, BANK), slice(BANK, J))
        whole = slice(0, J)
        for u in (0, 2, 1):
            gate(u)
        product(0)
        back(0)
        codes.append(keep.tile([P, 2 * widths[2]], U32, name="codes2", tag="first", align_bytes=64))
        quantize(2)
        after = shared.tile([P, J], F32, name="after", align_bytes=64, offset=4 * SPAN)
        result[0] = after[:]
        add_res(0, halves[0], nc.gpsimd)
        product(1)
        back(1)
        add_res(0, halves[1], nc.gpsimd)
        store(0, whole)
        product(2)

        last = len(units) - 1
        ahead = 3
        for u in range(2, last + 1):
            while ahead <= min(u + (1 if u < 6 else LEAD), last):
                front(ahead)
                ahead += 1
            if u == 13:
                add_res_turned(5, 0)
                store(5, halves[0])
            back(u)
            nt, jh = units[u]
            if u in (11, 12):
                add_res(nt, halves[jh], nc.gpsimd)
                store(nt, halves[jh])
            elif u < last - 3 and jh == 1:
                add_res(nt, whole, nc.gpsimd)
                if nt in (2, 4):
                    store_pair(nt // 2)
        for nt, jh in units[last - 2 :]:
            add_res(nt, halves[jh], nc.vector)
            store(nt, halves[jh])
